import numpy as np
CORES = [32,33,34,35,40,41,42,43]
N = 8
ROOT = 1
def setup_inputs(rng):
    return {"x": rng.standard_normal((N, 128, N * 128), dtype=np.float32)}
def reference(x):
    return {"y": np.stack([x[ROOT][:, r * 128:(r + 1) * 128] for r in range(N)])}

from concourse.bass import DstId, RemoteDMATransfer

W = 128

SCRATCH = {
    "stage": ("dram", [8, 128, W], "float32"),
    "rbuf": ("dram", [128, W], "float32"),
    "land": ("dram", [128, W], "float32"),
}
SEMAPHORES = ["lda", "ldb", "ldc", "own", "sent", "rin", "arrived", "stored"]


def plan(T, topo):
    cores = list(T.cores)
    root = cores[T.root] if T.root < len(cores) else T.root
    near = [c for c in cores if c != root and topo.chip(c) == topo.chip(root)]
    far = [c for c in cores if topo.chip(c) != topo.chip(root)]
    base = topo.chip(root) * 8
    ports = [c for c in range(base, base + 8) if c != root and topo.may_write(c, far[0])]
    d_a = [c for c in ports if topo.die(c) == topo.die(root)]
    d_b = [c for c in ports if topo.die(c) != topo.die(root)]
    relays = [d_a[0], d_b[0], d_a[1], d_b[1]]
    return cores, root, near, far, relays


def rank_program(g, core, T, topo):
    cores, root, near, far, relays = plan(T, topo)
    S = T.sem

    def xfer(dst, src_ap, dst_ap, mask, sem):
        rid, pid, _se = topo.addr(dst)
        return RemoteDMATransfer(dst_ids=[DstId(rid=rid, pnc=pid)], dma_engine_mask=mask, remote_sem=sem,
                                 src=src_ap, dst=dst_ap)

    if core == root:
        def cut(q, dst_core, sem):
            b = cores.index(dst_core)
            q.dma_start(T.stage[b], T.x[:, b * W:(b + 1) * W]).then_inc(sem, 16)

        def blk(dst_core):
            return T.stage[cores.index(dst_core)]

        cut(g.sync, far[0], S.lda)
        cut(g.scalar, far[1], S.lda)
        cut(g.sync, far[2], S.ldb)
        cut(g.scalar, far[3], S.ldb)
        g.sync.wait_ge(S.lda, 32)
        cut(g.sync, near[0], S.ldc)
        g.sync.wait_ge(S.ldb, 32)
        cut(g.sync, near[2], S.ldc)
        g.scalar.wait_ge(S.ldb, 32)
        cut(g.scalar, near[1], S.ldc)
        r = cores.index(root)
        g.scalar.dma_start(T.y[:, :], T.x[:, r * W:(r + 1) * W]).then_inc(S.own, 16)

        g.wait_ge(S.lda, 32)
        g.remote_dma_fused([xfer(relays[0], blk(far[0]), T.rbuf[:, :], 0x00FF, S.rin),
                            xfer(relays[1], blk(far[1]), T.rbuf[:, :], 0xFF00, S.rin)], local_sem=S.sent)
        g.wait_ge(S.ldb, 32)
        g.remote_dma_fused([xfer(relays[2], blk(far[2]), T.rbuf[:, :], 0x00FF, S.rin),
                            xfer(relays[3], blk(far[3]), T.rbuf[:, :], 0xFF00, S.rin)], local_sem=S.sent)
        g.wait_ge(S.ldc, 48)
        g.remote_dma_fused([xfer(near[0], blk(near[0]), T.land[:, :], 0x00FF, S.arrived),
                            xfer(near[1], blk(near[1]), T.land[:, :], 0x0F00, S.arrived),
                            xfer(near[2], blk(near[2]), T.land[:, :], 0xF000, S.arrived)], local_sem=S.sent)
        g.wait_ge(S.sent, 48)
        g.wait_ge(S.own, 16)
        return

    if core in near or core in far:
        n_in = 8 if (core in far or core == near[0]) else 4
        g.sync.wait_ge(S.arrived, n_in)
        g.sync.dma_start(T.y[:, :], T.land[:, :]).then_inc(S.stored, 16)

    if core in relays:
        dst = far[relays.index(core)]
        rid, pid, _se = topo.addr(dst)
        g.wait_ge(S.rin, 8)
        g.remote_dma(T.land[:, :], T.rbuf[:, :], S.arrived, S.sent, pid, rid, 0x00FF)
        g.wait_ge(S.sent, 8)

    if core in near or core in far:
        g.wait_ge(S.stored, 16)
